import numpy as np
import ml_dtypes

BF16 = ml_dtypes.bfloat16


def bf(x):
    return np.asarray(x, np.float32).astype(BF16)


def f32(x):
    return np.asarray(x, np.float32)


def f64(x):
    return np.asarray(x).astype(np.float64)


def striped(idx):
    return np.tile(idx.reshape(-1, 16).T, (8, 1))


S, K, M, N, D, V = 2048, 128, 256, 4096, 2, 2048


def setup_inputs():
    return {"table": bf(np.random.standard_normal((K, S))), "w": bf(np.random.standard_normal((D, K, M)) / np.sqrt(D * K)), "b": f32(0.5 * np.random.standard_normal((M, 1))), "offs": striped(np.random.permutation(np.tile(np.arange(S), 2))[:N])}


def reference(table, w, b, offs):
    idx = offs[:16].T.reshape(-1)
    x = f64(table)[:, idx]
    y = sum(f64(w)[t].T @ x[:, t * V : (t + 1) * V] for t in range(D))
    return np.maximum(y + f64(b), 0.0)

@@ -1,0 +1,49 @@
+import concourse.mybir as mybir
+
+BF16, F32, U16 = mybir.dt.bfloat16, mybir.dt.float32, mybir.dt.uint16
+ADD, MAX = mybir.AluOpType.add, mybir.AluOpType.max
+RELU = mybir.ActivationFunctionType.Relu
+
+P = 128
+NODES = 2048
+EDGES = 2048
+ENDS = 2
+M = 256
+BANK = 512
+PER_COLUMN = 16
+
+FLOPS = 2 * ENDS * P * M * EDGES
+
+
+def tile_gather_matmul_kernel(tc, table, w, b, offs, out):
+    nc = tc.nc
+    with (
+        tc.tile_pool(name="held", bufs=1) as held,
+        tc.tile_pool(name="results", bufs=8) as results,
+        tc.psum_pool(name="sums", bufs=8) as sums,
+    ):
+        nodes = held.tile([P, NODES], BF16, name="nodes")
+        weights = held.tile([P, ENDS, M], BF16, name="weights")
+        bias = held.tile([P, M // P], F32, name="bias")
+        offsets = held.tile([P, ENDS * EDGES // PER_COLUMN], U16, name="offsets")
+        nc.sync.dma_start(nodes[:], table)
+        nc.sync.dma_start(offsets[:], offs)
+        nc.scalar.dma_start(weights[:], w.rearrange("t k m -> k t m"))
+        nc.scalar.dma_start(bias[:], b.rearrange("(a p) o -> p (a o)", p=P))
+
+        for piece in range(EDGES // BANK):
+            for block in range(M // P):
+                rows = slice(block * P, (block + 1) * P)
+                bank = sums.tile([P, BANK], F32, name="bank")
+                for end in range(ENDS):
+                    first = (end * EDGES + piece * BANK) // PER_COLUMN
+                    picked = nodes[:].indirect(offsets[:, first : first + BANK // PER_COLUMN])
+                    nc.tensor.matmul(
+                        bank[:], weights[:, end, rows], picked, start=end == 0, stop=end == ENDS - 1
+                    )
+                result = results.tile([P, BANK], F32, name="result")
+                if block == 0:
+                    nc.vector.tensor_scalar(result[:], bank[:], bias[:, block : block + 1], 0.0, ADD, MAX)
+                else:
+                    nc.scalar.activation(result[:], bank[:], RELU, bias=bias[:, block : block + 1])
+                nc.sync.dma_start(out[rows, piece * BANK : (piece + 1) * BANK], result[:])

@@ -2,7 +2,6 @@ import concourse.mybir as mybir
 
 BF16, F32, U16 = mybir.dt.bfloat16, mybir.dt.float32, mybir.dt.uint16
 ADD, MAX = mybir.AluOpType.add, mybir.AluOpType.max
-RELU = mybir.ActivationFunctionType.Relu
 
 P = 128
 NODES = 2048
@@ -42,8 +41,5 @@ def tile_gather_matmul_kernel(tc, table, w, b, offs, out):
                         bank[:], weights[:, end, rows], picked, start=end == 0, stop=end == ENDS - 1
                     )
                 result = results.tile([P, BANK], F32, name="result")
-                if block == 0:
-                    nc.vector.tensor_scalar(result[:], bank[:], bias[:, block : block + 1], 0.0, ADD, MAX)
-                else:
-                    nc.scalar.activation(result[:], bank[:], RELU, bias=bias[:, block : block + 1])
+                nc.vector.tensor_scalar(result[:], bank[:], bias[:, block : block + 1], 0.0, ADD, MAX)
                 nc.sync.dma_start(out[rows, piece * BANK : (piece + 1) * BANK], result[:])

import concourse.mybir as mybir

BF16, F32, U16 = mybir.dt.bfloat16, mybir.dt.float32, mybir.dt.uint16
ADD, MAX = mybir.AluOpType.add, mybir.AluOpType.max

P = 128
NODES = 2048
EDGES = 2048
ENDS = 2
M = 256
BANK = 512
PER_COLUMN = 16

FLOPS = 2 * ENDS * P * M * EDGES


def tile_gather_matmul_kernel(tc, table, w, b, offs, out):
    nc = tc.nc
    with (
        tc.tile_pool(name="held", bufs=1) as held,
        tc.tile_pool(name="results", bufs=8) as results,
        tc.psum_pool(name="sums", bufs=8) as sums,
    ):
        nodes = held.tile([P, NODES], BF16, name="nodes")
        weights = held.tile([P, ENDS, M], BF16, name="weights")
        bias = held.tile([P, M // P], F32, name="bias")
        offsets = held.tile([P, ENDS * EDGES // PER_COLUMN], U16, name="offsets")
        nc.sync.dma_start(nodes[:], table)
        nc.sync.dma_start(offsets[:], offs)
        nc.scalar.dma_start(weights[:], w.rearrange("t k m -> k t m"))
        nc.scalar.dma_start(bias[:], b.rearrange("(a p) o -> p (a o)", p=P))

        for piece in range(EDGES // BANK):
            for block in range(M // P):
                rows = slice(block * P, (block + 1) * P)
                bank = sums.tile([P, BANK], F32, name="bank")
                for end in range(ENDS):
                    first = (end * EDGES + piece * BANK) // PER_COLUMN
                    picked = nodes[:].indirect(offsets[:, first : first + BANK // PER_COLUMN])
                    nc.tensor.matmul(
                        bank[:], weights[:, end, rows], picked, start=end == 0, stop=end == ENDS - 1
                    )
                result = results.tile([P, BANK], F32, name="result")
                nc.vector.tensor_scalar(result[:], bank[:], bias[:, block : block + 1], 0.0, ADD, MAX)
                nc.sync.dma_start(out[rows, piece * BANK : (piece + 1) * BANK], result[:])
